import numpy as np
import ml_dtypes


def mxq(x, axis, fmt="e4m3"):
    dtype, down = {"e4m3": (ml_dtypes.float8_e4m3fn, 7), "e5m2": (ml_dtypes.float8_e5m2, 14)}[fmt]
    v = np.moveaxis(np.asarray(x, np.float32).astype(ml_dtypes.bfloat16).astype(np.float64), axis, -1)
    blocks = v.reshape(v.shape[:-1] + (-1, 32))
    amax = np.abs(blocks).max(-1, keepdims=True)
    byte = np.maximum(np.where(amax > 0, np.frexp(amax)[1] - 1 + 127, 0) - down, 1)
    scale = np.exp2(byte - 127.0)
    codes = (blocks / scale).astype(np.float32).astype(dtype).astype(np.float64)
    return np.moveaxis((codes * scale).reshape(v.shape), -1, axis)


WIDE = False


def mx_kscale(k):
    if not WIDE:
        return np.ones(k)
    levels = np.array([30, -30])
    if k % 512:
        return np.exp2(np.random.permutation(np.resize(levels, k // 32))).repeat(32)
    a = np.empty((k // 512, 16))
    for p in range(k // 512):
        a[p, :8] = np.random.permutation(np.resize(levels, 8))
        for g in range(8):
            far = levels[np.abs(levels - a[p, g]) >= 10]
            a[p, g + 8] = far[np.random.randint(len(far))]
    return np.exp2(a.ravel()).repeat(32)


def f64(x):
    return np.asarray(x).astype(np.float64)


def striped(idx):
    return np.tile(np.asarray(idx).reshape(-1, 16).T, (8, 1)).astype(np.uint16)


def unstriped(offs):
    return offs[:16].T.reshape(-1).astype(np.int64)


E2M1 = np.array([0.0, 0.5, 1.0, 1.5, 2.0, 3.0, 4.0, 6.0, -0.0, -0.5, -1.0, -1.5, -2.0, -3.0, -4.0, -6.0])


def pack_weight(w, fmt):
    k, n = w.shape
    w = f64(np.asarray(w, np.float32).astype(ml_dtypes.bfloat16)).reshape(k // 32, 32, n)
    amax = np.abs(w).max(1)
    if fmt == "e4m3":
        byte = np.frexp(amax)[1] - 1 + 127 - 7
    else:
        mant, ex = np.frexp(amax / 6.0)
        byte = np.where(mant > 0.5, ex, ex - 1) + 127
    byte = np.clip(np.where(amax > 0, byte, 1), 1, 254)
    scaled = (w * np.exp2(127.0 - byte)[:, None, :]).reshape(k, n).astype(np.float32)
    by_word = np.ascontiguousarray(scaled.reshape(k // 512, 128, 4, n).transpose(0, 1, 3, 2))
    if fmt == "e4m3":
        words = by_word.astype(ml_dtypes.float8_e4m3fn).view(np.uint8)
    else:
        c = by_word.astype(ml_dtypes.float4_e2m1fn).view(np.uint8) & 0xF
        words = (c[..., 0::2] | (c[..., 1::2] << 4)).reshape(k // 512, 128, 2 * n)
    return np.ascontiguousarray(words), np.ascontiguousarray(byte.astype(np.uint8).reshape(k // 512, 16, n))


def unpack_weight(words, scales, fmt):
    g, _, n = scales.shape
    words = np.ascontiguousarray(words).reshape(g, 128, n, -1)
    if fmt == "e4m3":
        vals = words.view(ml_dtypes.float8_e4m3fn).astype(np.float64)
    else:
        nib = np.empty((g, 128, n, 4), np.uint8)
        nib[..., 0::2] = words & 0xF
        nib[..., 1::2] = words >> 4
        vals = E2M1[nib]
    vals = vals * np.repeat(np.exp2(scales.astype(np.float64) - 127.0), 8, axis=1)[..., None]
    return vals.transpose(0, 1, 3, 2).reshape(g * 512, n)


K, T, J, I, V = 1024, 1024, 256, 256, 1024


def setup_inputs():
    n = np.random.standard_normal
    idx = np.random.permutation(T)[:J]
    idx2 = np.random.permutation(V)[:I]
    fk = mx_kscale(K)
    xtp = pack_weight(n((K, T)) * 0.04 * fk[:, None], "e2m1")
    return {
        "xt_words": xtp[0],
        "xt_scales": xtp[1],
        "kf": (n((K, V))).astype(np.float32),
        "ko": (n((K, I)) * 0.6).astype(np.float32),
        "fi": (np.random.uniform(0.5, 2.0, (K, 1)) / fk[:, None]).astype(np.float32),
        "bi": (np.random.uniform(-0.7, 0.7, (1, I))).astype(np.float32),
        "tg": (np.random.uniform(-0.5, 1.5, (J, 1))).astype(np.float32),
        "offs": striped(idx),
        "offs2": striped(idx2),
    }


def reference(xt_words, xt_scales, kf, ko, fi, bi, tg, offs, offs2):
    idx = unstriped(offs)
    idx2 = unstriped(offs2)
    xtu = unpack_weight(xt_words, xt_scales, "e2m1")
    vk = (f64(kf)[:, idx2] + f64(ko)) * f64(fi)
    xtidxg = xtu[:, idx]
    vkq = mxq(vk, 0, "e5m2")
    a0 = xtidxg.T @ vkq
    a = a0 + f64(bi)
    y = np.square(np.maximum(a - f64(tg), 0.0))
    return y

@@ -1,0 +1,134 @@
+from contextlib import ExitStack
+
+import concourse.mybir as mybir
+from concourse.masks import make_identity
+
+K, T, J, I, V = 1024, 1024, 256, 256, 1024
+FLOPS = 2 * K * J * I
+
+F32 = mybir.dt.float32
+BF16 = mybir.dt.bfloat16
+I32 = mybir.dt.int32
+U32 = mybir.dt.uint32
+U16 = mybir.dt.uint16
+U8 = mybir.dt.uint8
+E5M2X4 = mybir.dt.float8_e5m2_x4
+E2M1X4 = mybir.dt.float4_e2m1fn_x4
+ALU = mybir.AluOpType
+ACT = mybir.ActivationFunctionType
+
+P = 128
+PACK = 4
+PASSES = K // (P * PACK)
+HALVES = J // P
+
+
+def tile_list_scores_picked_mixed_hinge_kernel(tc, xt_words, xt_scales, kf, ko, fi, bi, tg, offs, offs2, out):
+    nc = tc.nc
+    with ExitStack() as ctx:
+        sb = ctx.enter_context(tc.tile_pool(name="sb", bufs=1))
+        ps = ctx.enter_context(tc.psum_pool(name="ps", bufs=1))
+
+        tok_list = sb.tile([P, J // 16], U16, name="tok_list")
+        key_list = sb.tile([P, I // 16], U16, name="key_list")
+        store = [[sb.tile([P, V], F32, name=f"store{z}{t}") for t in range(PACK)] for z in range(PASSES)]
+        own = [sb.tile([P, PACK, I], F32, name=f"own{z}") for z in range(PASSES)]
+        words = [sb.tile([P, T], U16, name=f"words{z}") for z in range(PASSES)]
+        sc_rows = sb.tile([P, PASSES, T], U8, name="sc_rows")
+        fac = sb.tile([P, PASSES, PACK], F32, name="fac")
+        target = sb.tile([P, HALVES], F32, name="target")
+        bias_col = sb.tile([P, HALVES], F32, name="bias_col")
+        ident = sb.tile([P, P], F32, name="ident")
+        bias = sb.tile([P, I], F32, name="bias")
+
+        kf_v = kf.rearrange("(z p t) v -> z t p v", z=PASSES, t=PACK)
+        ko_v = ko.rearrange("(z p t) i -> z p t i", z=PASSES, t=PACK)
+
+        nc.vector.memset(sc_rows[:].rearrange("p z c -> p (z c)").bitcast(I32), 0)
+        make_identity(nc, ident[:])
+
+        nc.sync.dma_start(key_list[:], offs2)
+        nc.sync.dma_start(store[0][0][:], kf_v[0, 0])
+        nc.scalar.dma_start(fac[:], fi.rearrange("(z p t) o -> p z (t o)", z=PASSES, t=PACK))
+        with nc.allow_non_contiguous_dma(reason="one value a partition"):
+            nc.scalar.dma_start(target[:], tg.rearrange("(h p) o -> p (h o)", p=P))
+            nc.scalar.dma_start(bias_col[:], bi.rearrange("o (h p) -> p (o h)", p=P))
+        nc.sync.dma_start(own[0][:], ko_v[0])
+        for t in range(1, PACK):
+            nc.sync.dma_start(store[0][t][:], kf_v[0, t])
+        for q in range(4):
+            nc.sync.dma_start(
+                sc_rows[32 * q : 32 * q + 4].bitcast(I32),
+                xt_scales[:, 4 * q : 4 * q + 4, :].rearrange("z r c -> r z c").bitcast(I32),
+            )
+        nc.sync.dma_start(tok_list[:], offs)
+        nc.sync.dma_start(store[1][0][:], kf_v[1, 0])
+        nc.sync.dma_start(own[1][:], ko_v[1])
+        for t in range(1, PACK):
+            nc.sync.dma_start(store[1][t][:], kf_v[1, t])
+        for z in range(PASSES):
+            nc.sync.dma_start(words[z][:].bitcast(I32), xt_words[z].bitcast(I32))
+
+        bias_ps = ps.tile([P, I], F32, name="bias_ps")
+        for h in range(HALVES):
+            nc.tensor.transpose(bias_ps[:, h * P : (h + 1) * P], bias_col[:, h : h + 1].to_broadcast([P, P]), ident[:])
+        nc.scalar.copy(bias[:], bias_ps[:])
+
+        summed = [[[sb.tile([P, P], F32, name=f"summed{z}{t}{c}") for c in range(HALVES)] for t in range(PACK)] for z in range(PASSES)]
+        grouped = [[sb.tile([P, P, PACK], BF16, name=f"grouped{z}{c}", align_bytes=64) for c in range(HALVES)] for z in range(PASSES)]
+        k_codes = [sb.tile([P, I], U32, name=f"k_codes{z}", align_bytes=64) for z in range(PASSES)]
+        k_scales = [sb.tile([P, I], U8, name=f"k_scales{z}", align_bytes=64) for z in range(PASSES)]
+        x_codes = [[sb.tile([P, P], U16, name=f"x_codes{z}{h}", align_bytes=64) for h in range(HALVES)] for z in range(PASSES)]
+        x_scales = [sb.tile([P, J], U8, name=f"x_scales{z}", align_bytes=64) for z in range(PASSES)]
+        acc = [ps.tile([P, I], F32, name=f"acc{h}") for h in range(HALVES)]
+
+        def keys(z, t, c):
+            nc.vector.tensor_tensor(
+                summed[z][t][c][:],
+                store[z][t][:].indirect(key_list[:, c * 8 : (c + 1) * 8]),
+                own[z][:, t, c * P : (c + 1) * P],
+                ALU.add,
+            )
+            nc.scalar.activation(grouped[z][c][:, :, t], summed[z][t][c][:], ACT.Copy, scale=fac[:, z, t : t + 1])
+
+        def quantise(z, c):
+            nc.vector.quantize_mx(
+                out=k_codes[z][:, c * P : (c + 1) * P].bitcast(E5M2X4),
+                scales=k_scales[z][:, c * P : (c + 1) * P],
+                in_=grouped[z][c][:].rearrange("p c t -> p (c t)"),
+            )
+
+        def tokens(z, h):
+            nc.vector.tensor_copy(x_codes[z][h][:], words[z][:].indirect(tok_list[:, h * 8 : (h + 1) * 8]))
+
+        def product(z, h):
+            nc.tensor.matmul_mx(
+                out=acc[h][:],
+                lhsT=x_codes[z][h][:].bitcast(E2M1X4),
+                lhsT_scale=x_scales[z][:, h * P : (h + 1) * P],
+                rhs=k_codes[z][:].bitcast(E5M2X4),
+                rhs_scale=k_scales[z][:],
+                start=(z == 0),
+                stop=(z == PASSES - 1),
+            )
+
+        for z in range(PASSES):
+            nc.vector.tensor_copy(x_scales[z][:], sc_rows[:, z, :].indirect(tok_list[:]))
+        for z in range(PASSES):
+            for t in range(PACK):
+                for c in range(HALVES):
+                    keys(z, t, c)
+        for z in range(PASSES):
+            for c in range(HALVES):
+                quantise(z, c)
+            for h in range(HALVES):
+                tokens(z, h)
+                product(z, h)
+
+        excess = [sb.tile([P, I], F32, name=f"excess{h}") for h in range(HALVES)]
+        result = [sb.tile([P, I], F32, name=f"result{h}") for h in range(HALVES)]
+        for h in range(HALVES):
+            nc.vector.scalar_tensor_tensor(excess[h][:], acc[h][:], target[:, h : h + 1], bias[:], ALU.subtract, ALU.add)
+        for h, queue in enumerate((nc.sync, nc.scalar)):
+            nc.vector.scalar_tensor_tensor(result[h][:], excess[h][:], 0.0, excess[h][:], ALU.max, ALU.mult)
+            queue.dma_start(out[h * P : (h + 1) * P, :], result[h][:])

@@ -35,33 +35,31 @@ def tile_list_scores_picked_mixed_hinge_kernel(tc, xt_words, xt_scales, kf, ko, 
         own = [sb.tile([P, PACK, I], F32, name=f"own{z}") for z in range(PASSES)]
         words = [sb.tile([P, T], U16, name=f"words{z}") for z in range(PASSES)]
         sc_rows = sb.tile([P, PASSES, T], U8, name="sc_rows")
-        fac = sb.tile([P, PASSES, PACK], F32, name="fac")
-        target = sb.tile([P, HALVES], F32, name="target")
-        bias_col = sb.tile([P, HALVES], F32, name="bias_col")
+        rows = sb.tile([P, P * PACK], F32, name="rows")
+        fac = sb.tile([P, PACK, PASSES], F32, name="fac")
+        cols = sb.tile([P, 2 * HALVES], F32, name="cols")
         ident = sb.tile([P, P], F32, name="ident")
         bias = sb.tile([P, I], F32, name="bias")
 
         kf_v = kf.rearrange("(z p t) v -> z t p v", z=PASSES, t=PACK)
         ko_v = ko.rearrange("(z p t) i -> z p t i", z=PASSES, t=PACK)
 
-        nc.vector.memset(sc_rows[:].rearrange("p z c -> p (z c)").bitcast(I32), 0)
+        nc.vector.memset(sc_rows[0:112].rearrange("p z c -> p (z c)").bitcast(I32), 0)
+        nc.gpsimd.memset(rows[0:122, 0:P], 0.0)
+        nc.gpsimd.memset(rows[0:126, P:], 0.0)
         make_identity(nc, ident[:])
 
         nc.sync.dma_start(key_list[:], offs2)
         nc.sync.dma_start(store[0][0][:], kf_v[0, 0])
-        nc.scalar.dma_start(fac[:], fi.rearrange("(z p t) o -> p z (t o)", z=PASSES, t=PACK))
-        with nc.allow_non_contiguous_dma(reason="one value a partition"):
-            nc.scalar.dma_start(target[:], tg.rearrange("(h p) o -> p (h o)", p=P))
-            nc.scalar.dma_start(bias_col[:], bi.rearrange("o (h p) -> p (o h)", p=P))
+        nc.scalar.dma_start(rows[126:128, :], fi.rearrange("(z k) o -> z (k o)", z=PASSES))
+        nc.scalar.dma_start(rows[122:124, 0:P], tg.rearrange("(h p) o -> h (p o)", p=P))
+        nc.scalar.dma_start(rows[124:126, 0:P], bi.rearrange("o (h p) -> (o h) p", p=P))
+        nc.scalar.dma_start(sc_rows[112:P].bitcast(I32), xt_scales.rearrange("z r c -> r z c").bitcast(I32))
         nc.sync.dma_start(own[0][:], ko_v[0])
-        for t in range(1, PACK):
-            nc.sync.dma_start(store[0][t][:], kf_v[0, t])
-        for q in range(4):
-            nc.sync.dma_start(
-                sc_rows[32 * q : 32 * q + 4].bitcast(I32),
-                xt_scales[:, 4 * q : 4 * q + 4, :].rearrange("z r c -> r z c").bitcast(I32),
-            )
+        nc.sync.dma_start(store[0][1][:], kf_v[0, 1])
         nc.sync.dma_start(tok_list[:], offs)
+        for t in range(2, PACK):
+            nc.sync.dma_start(store[0][t][:], kf_v[0, t])
         nc.sync.dma_start(store[1][0][:], kf_v[1, 0])
         nc.sync.dma_start(own[1][:], ko_v[1])
         for t in range(1, PACK):
@@ -69,9 +67,16 @@ def tile_list_scores_picked_mixed_hinge_kernel(tc, xt_words, xt_scales, kf, ko, 
         for z in range(PASSES):
             nc.sync.dma_start(words[z][:].bitcast(I32), xt_words[z].bitcast(I32))
 
+        fac_ps = ps.tile([P, PACK, P], F32, name="fac_ps")
+        for t in range(PACK):
+            nc.tensor.transpose(fac_ps[:, t, :], rows[:, t : P * PACK : PACK], ident[:])
+        nc.scalar.copy(fac[:], fac_ps[:, :, 126:128])
+        cols_ps = ps.tile([P, P], F32, name="cols_ps")
+        nc.tensor.transpose(cols_ps[:], rows[:, 0:P], ident[:])
+        nc.scalar.copy(cols[:], cols_ps[:, 122:126])
         bias_ps = ps.tile([P, I], F32, name="bias_ps")
         for h in range(HALVES):
-            nc.tensor.transpose(bias_ps[:, h * P : (h + 1) * P], bias_col[:, h : h + 1].to_broadcast([P, P]), ident[:])
+            nc.tensor.transpose(bias_ps[:, h * P : (h + 1) * P], cols[:, 2 + h : 3 + h].to_broadcast([P, P]), ident[:])
         nc.scalar.copy(bias[:], bias_ps[:])
 
         summed = [[[sb.tile([P, P], F32, name=f"summed{z}{t}{c}") for c in range(HALVES)] for t in range(PACK)] for z in range(PASSES)]
@@ -79,7 +84,8 @@ def tile_list_scores_picked_mixed_hinge_kernel(tc, xt_words, xt_scales, kf, ko, 
         k_codes = [sb.tile([P, I], U32, name=f"k_codes{z}", align_bytes=64) for z in range(PASSES)]
         k_scales = [sb.tile([P, I], U8, name=f"k_scales{z}", align_bytes=64) for z in range(PASSES)]
         x_codes = [[sb.tile([P, P], U16, name=f"x_codes{z}{h}", align_bytes=64) for h in range(HALVES)] for z in range(PASSES)]
-        x_scales = [sb.tile([P, J], U8, name=f"x_scales{z}", align_bytes=64) for z in range(PASSES)]
+        picked = sb.tile([P, PASSES, J], U8, name="picked")
+        x_scales = sb.tile([P, PASSES, J], U8, name="x_scales", align_bytes=64)
         acc = [ps.tile([P, I], F32, name=f"acc{h}") for h in range(HALVES)]
 
         def keys(z, t, c):
@@ -89,7 +95,7 @@ def tile_list_scores_picked_mixed_hinge_kernel(tc, xt_words, xt_scales, kf, ko, 
                 own[z][:, t, c * P : (c + 1) * P],
                 ALU.add,
             )
-            nc.scalar.activation(grouped[z][c][:, :, t], summed[z][t][c][:], ACT.Copy, scale=fac[:, z, t : t + 1])
+            nc.scalar.activation(grouped[z][c][:, :, t], summed[z][t][c][:], ACT.Copy, scale=fac[:, t, z : z + 1])
 
         def quantise(z, c):
             nc.vector.quantize_mx(
@@ -105,7 +111,7 @@ def tile_list_scores_picked_mixed_hinge_kernel(tc, xt_words, xt_scales, kf, ko, 
             nc.tensor.matmul_mx(
                 out=acc[h][:],
                 lhsT=x_codes[z][h][:].bitcast(E2M1X4),
-                lhsT_scale=x_scales[z][:, h * P : (h + 1) * P],
+                lhsT_scale=x_scales[:, z, h * P : (h + 1) * P],
                 rhs=k_codes[z][:].bitcast(E5M2X4),
                 rhs_scale=k_scales[z][:],
                 start=(z == 0),
@@ -113,7 +119,12 @@ def tile_list_scores_picked_mixed_hinge_kernel(tc, xt_words, xt_scales, kf, ko, 
             )
 
         for z in range(PASSES):
-            nc.vector.tensor_copy(x_scales[z][:], sc_rows[:, z, :].indirect(tok_list[:]))
+            nc.vector.tensor_copy(picked[:, z, :], sc_rows[:, z, :].indirect(tok_list[:]))
+        picked_w = picked[:].rearrange("p z c -> p (z c)").bitcast(I32)
+        x_scales_w = x_scales[:].rearrange("p z c -> p (z c)").bitcast(I32)
+        nc.vector.memset(x_scales_w, 0)
+        for q in range(4):
+            nc.gpsimd.dma_start(x_scales_w[32 * q : 32 * q + 4], picked_w[112 + 4 * q : 116 + 4 * q])
         for z in range(PASSES):
             for t in range(PACK):
                 for c in range(HALVES):
@@ -128,7 +139,7 @@ def tile_list_scores_picked_mixed_hinge_kernel(tc, xt_words, xt_scales, kf, ko, 
         excess = [sb.tile([P, I], F32, name=f"excess{h}") for h in range(HALVES)]
         result = [sb.tile([P, I], F32, name=f"result{h}") for h in range(HALVES)]
         for h in range(HALVES):
-            nc.vector.scalar_tensor_tensor(excess[h][:], acc[h][:], target[:, h : h + 1], bias[:], ALU.subtract, ALU.add)
+            nc.vector.scalar_tensor_tensor(excess[h][:], acc[h][:], cols[:, h : h + 1], bias[:], ALU.subtract, ALU.add)
         for h, queue in enumerate((nc.sync, nc.scalar)):
             nc.vector.scalar_tensor_tensor(result[h][:], excess[h][:], 0.0, excess[h][:], ALU.max, ALU.mult)
             queue.dma_start(out[h * P : (h + 1) * P, :], result[h][:])

from contextlib import ExitStack

import concourse.mybir as mybir
from concourse.masks import make_identity

K, T, J, I, V = 1024, 1024, 256, 256, 1024
FLOPS = 2 * K * J * I

F32 = mybir.dt.float32
BF16 = mybir.dt.bfloat16
I32 = mybir.dt.int32
U32 = mybir.dt.uint32
U16 = mybir.dt.uint16
U8 = mybir.dt.uint8
E5M2X4 = mybir.dt.float8_e5m2_x4
E2M1X4 = mybir.dt.float4_e2m1fn_x4
ALU = mybir.AluOpType
ACT = mybir.ActivationFunctionType

P = 128
PACK = 4
PASSES = K // (P * PACK)
HALVES = J // P


def tile_list_scores_picked_mixed_hinge_kernel(tc, xt_words, xt_scales, kf, ko, fi, bi, tg, offs, offs2, out):
    nc = tc.nc
    with ExitStack() as ctx:
        sb = ctx.enter_context(tc.tile_pool(name="sb", bufs=1))
        ps = ctx.enter_context(tc.psum_pool(name="ps", bufs=1))

        tok_list = sb.tile([P, J // 16], U16, name="tok_list")
        key_list = sb.tile([P, I // 16], U16, name="key_list")
        store = [[sb.tile([P, V], F32, name=f"store{z}{t}") for t in range(PACK)] for z in range(PASSES)]
        own = [sb.tile([P, PACK, I], F32, name=f"own{z}") for z in range(PASSES)]
        words = [sb.tile([P, T], U16, name=f"words{z}") for z in range(PASSES)]
        sc_rows = sb.tile([P, PASSES, T], U8, name="sc_rows")
        rows = sb.tile([P, P * PACK], F32, name="rows")
        fac = sb.tile([P, PACK, PASSES], F32, name="fac")
        cols = sb.tile([P, 2 * HALVES], F32, name="cols")
        ident = sb.tile([P, P], F32, name="ident")
        bias = sb.tile([P, I], F32, name="bias")

        kf_v = kf.rearrange("(z p t) v -> z t p v", z=PASSES, t=PACK)
        ko_v = ko.rearrange("(z p t) i -> z p t i", z=PASSES, t=PACK)

        nc.vector.memset(sc_rows[0:112].rearrange("p z c -> p (z c)").bitcast(I32), 0)
        nc.gpsimd.memset(rows[0:122, 0:P], 0.0)
        nc.gpsimd.memset(rows[0:126, P:], 0.0)
        make_identity(nc, ident[:])

        nc.sync.dma_start(key_list[:], offs2)
        nc.sync.dma_start(store[0][0][:], kf_v[0, 0])
        nc.scalar.dma_start(rows[126:128, :], fi.rearrange("(z k) o -> z (k o)", z=PASSES))
        nc.scalar.dma_start(rows[122:124, 0:P], tg.rearrange("(h p) o -> h (p o)", p=P))
        nc.scalar.dma_start(rows[124:126, 0:P], bi.rearrange("o (h p) -> (o h) p", p=P))
        nc.scalar.dma_start(sc_rows[112:P].bitcast(I32), xt_scales.rearrange("z r c -> r z c").bitcast(I32))
        nc.sync.dma_start(own[0][:], ko_v[0])
        nc.sync.dma_start(store[0][1][:], kf_v[0, 1])
        nc.sync.dma_start(tok_list[:], offs)
        for t in range(2, PACK):
            nc.sync.dma_start(store[0][t][:], kf_v[0, t])
        nc.sync.dma_start(store[1][0][:], kf_v[1, 0])
        nc.sync.dma_start(own[1][:], ko_v[1])
        for t in range(1, PACK):
            nc.sync.dma_start(store[1][t][:], kf_v[1, t])
        for z in range(PASSES):
            nc.sync.dma_start(words[z][:].bitcast(I32), xt_words[z].bitcast(I32))

        fac_ps = ps.tile([P, PACK, P], F32, name="fac_ps")
        for t in range(PACK):
            nc.tensor.transpose(fac_ps[:, t, :], rows[:, t : P * PACK : PACK], ident[:])
        nc.scalar.copy(fac[:], fac_ps[:, :, 126:128])
        cols_ps = ps.tile([P, P], F32, name="cols_ps")
        nc.tensor.transpose(cols_ps[:], rows[:, 0:P], ident[:])
        nc.scalar.copy(cols[:], cols_ps[:, 122:126])
        bias_ps = ps.tile([P, I], F32, name="bias_ps")
        for h in range(HALVES):
            nc.tensor.transpose(bias_ps[:, h * P : (h + 1) * P], cols[:, 2 + h : 3 + h].to_broadcast([P, P]), ident[:])
        nc.scalar.copy(bias[:], bias_ps[:])

        summed = [[[sb.tile([P, P], F32, name=f"summed{z}{t}{c}") for c in range(HALVES)] for t in range(PACK)] for z in range(PASSES)]
        grouped = [[sb.tile([P, P, PACK], BF16, name=f"grouped{z}{c}", align_bytes=64) for c in range(HALVES)] for z in range(PASSES)]
        k_codes = [sb.tile([P, I], U32, name=f"k_codes{z}", align_bytes=64) for z in range(PASSES)]
        k_scales = [sb.tile([P, I], U8, name=f"k_scales{z}", align_bytes=64) for z in range(PASSES)]
        x_codes = [[sb.tile([P, P], U16, name=f"x_codes{z}{h}", align_bytes=64) for h in range(HALVES)] for z in range(PASSES)]
        picked = sb.tile([P, PASSES, J], U8, name="picked")
        x_scales = sb.tile([P, PASSES, J], U8, name="x_scales", align_bytes=64)
        acc = [ps.tile([P, I], F32, name=f"acc{h}") for h in range(HALVES)]

        def keys(z, t, c):
            nc.vector.tensor_tensor(
                summed[z][t][c][:],
                store[z][t][:].indirect(key_list[:, c * 8 : (c + 1) * 8]),
                own[z][:, t, c * P : (c + 1) * P],
                ALU.add,
            )
            nc.scalar.activation(grouped[z][c][:, :, t], summed[z][t][c][:], ACT.Copy, scale=fac[:, t, z : z + 1])

        def quantise(z, c):
            nc.vector.quantize_mx(
                out=k_codes[z][:, c * P : (c + 1) * P].bitcast(E5M2X4),
                scales=k_scales[z][:, c * P : (c + 1) * P],
                in_=grouped[z][c][:].rearrange("p c t -> p (c t)"),
            )

        def tokens(z, h):
            nc.vector.tensor_copy(x_codes[z][h][:], words[z][:].indirect(tok_list[:, h * 8 : (h + 1) * 8]))

        def product(z, h):
            nc.tensor.matmul_mx(
                out=acc[h][:],
                lhsT=x_codes[z][h][:].bitcast(E2M1X4),
                lhsT_scale=x_scales[:, z, h * P : (h + 1) * P],
                rhs=k_codes[z][:].bitcast(E5M2X4),
                rhs_scale=k_scales[z][:],
                start=(z == 0),
                stop=(z == PASSES - 1),
            )

        for z in range(PASSES):
            nc.vector.tensor_copy(picked[:, z, :], sc_rows[:, z, :].indirect(tok_list[:]))
        picked_w = picked[:].rearrange("p z c -> p (z c)").bitcast(I32)
        x_scales_w = x_scales[:].rearrange("p z c -> p (z c)").bitcast(I32)
        nc.vector.memset(x_scales_w, 0)
        for q in range(4):
            nc.gpsimd.dma_start(x_scales_w[32 * q : 32 * q + 4], picked_w[112 + 4 * q : 116 + 4 * q])
        for z in range(PASSES):
            for t in range(PACK):
                for c in range(HALVES):
                    keys(z, t, c)
        for z in range(PASSES):
            for c in range(HALVES):
                quantise(z, c)
            for h in range(HALVES):
                tokens(z, h)
                product(z, h)

        excess = [sb.tile([P, I], F32, name=f"excess{h}") for h in range(HALVES)]
        result = [sb.tile([P, I], F32, name=f"result{h}") for h in range(HALVES)]
        for h in range(HALVES):
            nc.vector.scalar_tensor_tensor(excess[h][:], acc[h][:], cols[:, h : h + 1], bias[:], ALU.subtract, ALU.add)
        for h, queue in enumerate((nc.sync, nc.scalar)):
            nc.vector.scalar_tensor_tensor(result[h][:], excess[h][:], 0.0, excess[h][:], ALU.max, ALU.mult)
            queue.dma_start(out[h * P : (h + 1) * P, :], result[h][:])
